import numpy as np
import ml_dtypes


def mxq(x, axis, fmt="e4m3"):
    dtype, down = {"e4m3": (ml_dtypes.float8_e4m3fn, 7), "e5m2": (ml_dtypes.float8_e5m2, 14)}[fmt]
    v = np.moveaxis(np.asarray(x, np.float32).astype(ml_dtypes.bfloat16).astype(np.float64), axis, -1)
    blocks = v.reshape(v.shape[:-1] + (-1, 32))
    amax = np.abs(blocks).max(-1, keepdims=True)
    byte = np.maximum(np.where(amax > 0, np.frexp(amax)[1] - 1 + 127, 0) - down, 1)
    scale = np.exp2(byte - 127.0)
    codes = (blocks / scale).astype(np.float32).astype(dtype).astype(np.float64)
    return np.moveaxis((codes * scale).reshape(v.shape), -1, axis)


WIDE = False


def mx_kscale(k):
    if not WIDE:
        return np.ones(k)
    levels = np.array([30, -30])
    if k % 512:
        return np.exp2(np.random.permutation(np.resize(levels, k // 32))).repeat(32)
    a = np.empty((k // 512, 16))
    for p in range(k // 512):
        a[p, :8] = np.random.permutation(np.resize(levels, 8))
        for g in range(8):
            far = levels[np.abs(levels - a[p, g]) >= 10]
            a[p, g + 8] = far[np.random.randint(len(far))]
    return np.exp2(a.ravel()).repeat(32)


def f64(x):
    return np.asarray(x).astype(np.float64)


def striped(idx):
    return np.tile(np.asarray(idx).reshape(-1, 16).T, (8, 1)).astype(np.uint16)


def unstriped(offs):
    return offs[:16].T.reshape(-1).astype(np.int64)


E2M1 = np.array([0.0, 0.5, 1.0, 1.5, 2.0, 3.0, 4.0, 6.0, -0.0, -0.5, -1.0, -1.5, -2.0, -3.0, -4.0, -6.0])


def pack_weight(w, fmt):
    k, n = w.shape
    w = f64(np.asarray(w, np.float32).astype(ml_dtypes.bfloat16)).reshape(k // 32, 32, n)
    amax = np.abs(w).max(1)
    if fmt in ("e4m3", "e5m2"):
        byte = np.frexp(amax)[1] - 1 + 127 - (7 if fmt == "e4m3" else 14)
    else:
        mant, ex = np.frexp(amax / 6.0)
        byte = np.where(mant > 0.5, ex, ex - 1) + 127
    byte = np.clip(np.where(amax > 0, byte, 1), 1, 254)
    scaled = (w * np.exp2(127.0 - byte)[:, None, :]).reshape(k, n).astype(np.float32)
    by_word = np.ascontiguousarray(scaled.reshape(k // 512, 128, 4, n).transpose(0, 1, 3, 2))
    if fmt in ("e4m3", "e5m2"):
        words = by_word.astype(ml_dtypes.float8_e4m3fn if fmt == "e4m3" else ml_dtypes.float8_e5m2).view(np.uint8)
    else:
        c = by_word.astype(ml_dtypes.float4_e2m1fn).view(np.uint8) & 0xF
        words = (c[..., 0::2] | (c[..., 1::2] << 4)).reshape(k // 512, 128, 2 * n)
    return np.ascontiguousarray(words), np.ascontiguousarray(byte.astype(np.uint8).reshape(k // 512, 16, n))


def unpack_weight(words, scales, fmt):
    g, _, n = scales.shape
    words = np.ascontiguousarray(words).reshape(g, 128, n, -1)
    if fmt in ("e4m3", "e5m2"):
        vals = words.view(ml_dtypes.float8_e4m3fn if fmt == "e4m3" else ml_dtypes.float8_e5m2).astype(np.float64)
    else:
        nib = np.empty((g, 128, n, 4), np.uint8)
        nib[..., 0::2] = words & 0xF
        nib[..., 1::2] = words >> 4
        vals = E2M1[nib]
    vals = vals * np.repeat(np.exp2(scales.astype(np.float64) - 127.0), 8, axis=1)[..., None]
    return vals.transpose(0, 1, 3, 2).reshape(g * 512, n)


def sigmoid(v):
    return 1.0 / (1.0 + np.exp(-v))


def sgn(shape):
    return np.random.uniform(0.5, 2.0, shape) * np.where(np.random.standard_normal(shape) < 0, -1.0, 1.0)


K, T, J, R, C, D, O, N = 512, 2048, 256, 512, 512, 512, 128, 256


def setup_inputs():
    n = np.random.standard_normal
    idx = np.random.permutation(T)[:J]
    idx2 = np.random.permutation(T)[:J]
    idx3 = np.random.permutation(C)[:J]
    idx4 = np.random.permutation(D)[:J]
    idx5 = np.random.permutation(C)[:O]
    idx6 = np.random.permutation(C)[:O]
    idx7 = np.random.permutation(D)[:O]
    fk = mx_kscale(K)
    fr = mx_kscale(R)
    xtp = pack_weight(n((K, T)) / fk[:, None], "e2m1")
    wp = pack_weight(n((K, R)) * 1 / np.sqrt(K) * fk[:, None], "e5m2")
    w2p = pack_weight(n((K, R)) * 1 / np.sqrt(K) * fk[:, None], "e4m3")
    wbp = pack_weight(n((R, N)) * 1 / np.sqrt(R) / fr[:, None], "e4m3")
    return {
        "xt_words": xtp[0],
        "xt_scales": xtp[1],
        "w_words": wp[0],
        "w_scales": wp[1],
        "w2_words": w2p[0],
        "w2_scales": w2p[1],
        "sa": (np.random.uniform(0.5, 1.6, (R, 1)) * fr[:, None]).astype(np.float32),
        "sb": (np.random.uniform(0.5, 1.6, (R, 1)) * fr[:, None]).astype(np.float32),
        "sg": (sgn((R, 1))).astype(np.float32),
        "bg": (np.random.uniform(-2.0, 2.0, (R, 1))).astype(np.float32),
        "wb_words": wbp[0],
        "wb_scales": wbp[1],
        "offs": striped(idx),
        "offs2": striped(idx2),
        "offs3": striped(idx3),
        "offs4": striped(idx4),
        "offs5": striped(idx5),
        "offs6": striped(idx6),
        "offs7": striped(idx7),
    }


def reference(xt_words, xt_scales, w_words, w_scales, w2_words, w2_scales, sa, sb, sg, bg, wb_words, wb_scales, offs, offs2, offs3, offs4, offs5, offs6, offs7):
    idx = unstriped(offs)
    idx2 = unstriped(offs2)
    idx3 = unstriped(offs3)
    idx4 = unstriped(offs4)
    idx5 = unstriped(offs5)
    idx6 = unstriped(offs6)
    idx7 = unstriped(offs7)
    xtu = unpack_weight(xt_words, xt_scales, "e2m1")
    wu = unpack_weight(w_words, w_scales, "e5m2")
    w2u = unpack_weight(w2_words, w2_scales, "e4m3")
    wbu = unpack_weight(wb_words, wb_scales, "e4m3")
    xtidxg = xtu[:, idx]
    a = wu.T @ xtidxg
    xtidx2g = xtu[:, idx2]
    b = w2u.T @ xtidx2g
    pw = np.zeros((R, C))
    pw[:, idx3] = a
    pv = np.zeros((R, D))
    pv[:, idx4] = b
    u1 = pw[:, idx5] * f64(sa) * sigmoid(pw[:, idx6] * f64(sg) + f64(bg))
    hid = np.maximum(u1, pv[:, idx7] * f64(sb))
    hidq = mxq(hid, 0, "e5m2")
    y = wbu.T @ hidq
    return y

@@ -1,0 +1,234 @@
+from contextlib import ExitStack
+
+import concourse.mybir as mybir
+
+K, T, J, R, C, O, N = 512, 2048, 256, 512, 512, 128, 256
+FLOPS = 2 * (2 * K * R * J + R * N * O)
+
+F32 = mybir.dt.float32
+BF16 = mybir.dt.bfloat16
+I32 = mybir.dt.int32
+U32 = mybir.dt.uint32
+U16 = mybir.dt.uint16
+U8 = mybir.dt.uint8
+E2M1 = mybir.dt.float4_e2m1fn_x4
+E4M3 = mybir.dt.float8_e4m3fn_x4
+E5M2 = mybir.dt.float8_e5m2_x4
+ACT = mybir.ActivationFunctionType
+ALU = mybir.AluOpType
+
+P = 128
+PACK = 4
+QUADS = 4
+QUAD = 32
+
+
+def tile_list_gatedboards_ahead_one_plain_kernel(
+    tc, xt_words, xt_scales, w_words, w_scales, w2_words, w2_scales, sa, sb, sg, bg,
+    wb_words, wb_scales, offs, offs2, offs3, offs4, offs5, offs6, offs7, out,
+):
+    nc = tc.nc
+
+    with ExitStack() as ctx:
+        keep = ctx.enter_context(tc.tile_pool(name="keep", bufs=1))
+        psum = ctx.enter_context(tc.psum_pool(name="psum", bufs=1))
+
+        def sbuf(name, shape, dtype, tag=None):
+            return keep.tile(shape, dtype, name=name, tag=tag or name, align_bytes=64)
+
+        def load_list(name, dram):
+            tile = keep.tile(list(dram.shape), U16, name=name)
+            nc.sync.dma_start(tile[:], dram)
+            return tile
+
+        def load_words(queue, tile, dram):
+            queue.dma_start(tile[:].bitcast(I32), dram[0].rearrange("p c t -> p (c t)").bitcast(I32))
+
+        def load_scale_rows(queue, plane, dram):
+            rows = dram[0].bitcast(I32)
+            for q in range(QUADS):
+                queue.dma_start(
+                    plane[QUAD * q : QUAD * q + PACK, :].bitcast(I32), rows[PACK * q : PACK * (q + 1), :]
+                )
+
+        def load_feature_vector(name, dram):
+            tile = keep.tile([P, PACK], F32, name=name)
+            nc.sync.dma_start(tile[:], dram.rearrange("(p t) one -> p (t one)", t=PACK))
+            return tile
+
+        def deal_words(dealt, words):
+            nc.scalar.copy(
+                out=dealt[:].rearrange("p (t c i) -> p c t i", t=PACK, i=4),
+                in_=words[:].rearrange("p (c i t) -> p c t i", t=PACK, i=4),
+            )
+
+        def deal_scales(dealt, plane):
+            nc.vector.tensor_copy(
+                out=dealt[:].rearrange("p (t c i) -> p c t i", t=PACK, i=16),
+                in_=plane[:].rearrange("p (c i t) -> p c t i", t=PACK, i=16),
+            )
+
+        xt_w = sbuf("xt_w", [P, T], U16)
+        xt_s = sbuf("xt_s", [P, T], U8)
+        w_w = sbuf("w_w", [P, R], U32)
+        w_stage = sbuf("w_stage", [PACK, QUADS, R // 4], I32)
+        w_s = sbuf("w_s", [P, R], U8)
+        w2_w = sbuf("w2_w", [P, R], U32)
+        w2_s = sbuf("w2_s", [P, R], U8, tag="w2_s_then_a0")
+        wb_w = sbuf("wb_w", [P, N], U32)
+        wb_s = sbuf("wb_s", [P, N], U8)
+        pw = [sbuf("pw%d" % i, [P, C], F32) for i in range(2)]
+        pv = [sbuf("pv%d" % i, [P, C], F32) for i in range(3)]
+
+        for plane in (xt_s, w_s, w2_s, wb_s):
+            nc.vector.memset(plane[:].bitcast(I32), 0)
+        for board in pw + pv:
+            nc.vector.memset(board[:], 0.0)
+
+        nc.sync.dma_start(w_stage[:], w_scales[0].bitcast(I32).rearrange("(q r) c -> r q c", r=PACK))
+        list1 = load_list("list1", offs)
+        load_words(nc.sync, w_w, w_words)
+        nc.sync.dma_start(xt_w[:].bitcast(I32), xt_words[0].bitcast(I32))
+        load_scale_rows(nc.scalar, xt_s, xt_scales)
+        list2 = load_list("list2", offs2)
+        load_words(nc.sync, w2_w, w2_words)
+        list3 = load_list("list3", offs3)
+        load_scale_rows(nc.sync, w2_s, w2_scales)
+        list6 = load_list("list6", offs6)
+        sg_t = load_feature_vector("sg_t", sg)
+        bg_t = load_feature_vector("bg_t", bg)
+        list5 = load_list("list5", offs5)
+        sa_t = load_feature_vector("sa_t", sa)
+        list4 = load_list("list4", offs4)
+        list7 = load_list("list7", offs7)
+        sb_t = load_feature_vector("sb_t", sb)
+        load_words(nc.sync, wb_w, wb_words)
+        load_scale_rows(nc.sync, wb_s, wb_scales)
+
+        for q in range(QUADS):
+            nc.vector.tensor_copy(out=w_s[QUAD * q : QUAD * q + PACK, :].bitcast(I32), in_=w_stage[:, q, :])
+        w_dw = sbuf("w_dw", [P, R], U32)
+        w_ds = sbuf("w_ds", [P, R], U8)
+        deal_scales(w_ds, w_s)
+        deal_words(w_dw, w_w)
+
+        def gather_tokens(name, offsets):
+            words = sbuf(name + "_w", [P, J], U16)
+            scales = sbuf(name + "_s", [P, J], U8)
+            nc.vector.tensor_copy(out=scales[:], in_=xt_s[:].indirect(offsets[:]))
+            nc.vector.tensor_copy(out=words[:], in_=xt_w[:].indirect(offsets[:]))
+            return words, scales
+
+        def product(out_rows, t, words, scales, fmt, x_w, x_s):
+            cols = slice(P * t, P * (t + 1))
+            nc.tensor.matmul_mx(
+                out=out_rows,
+                lhsT=words[:, cols].bitcast(fmt),
+                lhsT_scale=scales[:, cols],
+                rhs=x_w[:].bitcast(E2M1),
+                rhs_scale=x_s[:],
+                start=True,
+                stop=True,
+            )
+
+        def empty(engine, name, bank, tag=None):
+            rows = sbuf(name, list(bank.shape), F32, tag=tag)
+            if engine is nc.scalar:
+                nc.scalar.copy(out=rows[:], in_=bank[:])
+            else:
+                nc.vector.tensor_copy(out=rows[:], in_=bank[:])
+            return rows
+
+        def scatter(engine, board, offsets, values):
+            if engine is nc.scalar:
+                nc.scalar.activation(out=board[:].indirect(offsets[:]), in_=values, func=ACT.Copy)
+            else:
+                nc.vector.tensor_copy(out=board[:].indirect(offsets[:]), in_=values)
+
+        first = sbuf("first", [P, PACK, O], F32)
+        gate = sbuf("gate", [P, PACK, O], F32)
+        second = sbuf("second", [P, PACK, O], F32)
+
+        def fetch_pw(board, t):
+            nc.scalar.activation(
+                out=gate[:, t, :], in_=board[:].indirect(list6[:]), func=ACT.Sigmoid,
+                bias=bg_t[:, t : t + 1], scale=sg_t[:, t : t + 1],
+            )
+            nc.scalar.activation(
+                out=first[:, t, :], in_=board[:].indirect(list5[:]), func=ACT.Copy, scale=sa_t[:, t : t + 1]
+            )
+
+        def fetch_pv(board, t):
+            nc.scalar.activation(
+                out=second[:, t, :], in_=board[:].indirect(list7[:]), func=ACT.Copy, scale=sb_t[:, t : t + 1]
+            )
+
+        a0_bank = psum.tile([P, J], F32, name="a0_bank")
+        a1_bank = psum.tile([P, J], F32, name="a1_bank")
+        a3_bank = psum.tile([P, J], F32, name="a3_bank")
+        b01_bank = psum.tile([P, 2, J], F32, name="b01_bank")
+        b3_bank = psum.tile([P, J], F32, name="b3_bank")
+        a2b2_bank = psum.tile([P, 2, J], F32, name="a2b2_bank")
+
+        x1_w, x1_s = gather_tokens("x1", list1)
+        for t, rows in ((1, a1_bank[:]), (3, a3_bank[:]), (0, a0_bank[:]), (2, a2b2_bank[:, 0, :])):
+            product(rows, t, w_dw, w_ds, E5M2, x1_w, x1_s)
+
+        x2_w, x2_s = gather_tokens("x2", list2)
+        w2_dw = sbuf("w2_dw", [P, R], U32)
+        w2_ds = sbuf("w2_ds", [P, R], U8)
+        deal_words(w2_dw, w2_w)
+        deal_scales(w2_ds, w2_s)
+        for t, rows in ((0, b01_bank[:, 0, :]), (1, b01_bank[:, 1, :]), (3, b3_bank[:]), (2, a2b2_bank[:, 1, :])):
+            product(rows, t, w2_dw, w2_ds, E4M3, x2_w, x2_s)
+
+        a1 = empty(nc.scalar, "a1", a1_bank)
+        scatter(nc.scalar, pw[1], list3, a1[:])
+        a0 = empty(nc.vector, "a0", a0_bank, tag="w2_s_then_a0")
+        scatter(nc.vector, pw[0], list3, a0[:])
+        fetch_pw(pw[1], 1)
+        a3 = empty(nc.scalar, "a3", a3_bank)
+        scatter(nc.scalar, pw[1], list3, a3[:])
+        b01 = empty(nc.vector, "b01", b01_bank)
+        scatter(nc.vector, pv[0], list4, b01[:, 0, :])
+        fetch_pw(pw[1], 3)
+        fetch_pw(pw[0], 0)
+        scatter(nc.vector, pv[1], list4, b01[:, 1, :])
+        b3 = empty(nc.scalar, "b3", b3_bank)
+        a2b2 = empty(nc.scalar, "a2b2", a2b2_bank)
+        fetch_pv(pv[0], 0)
+        scatter(nc.scalar, pw[0], list3, a2b2[:, 0, :])
+        scatter(nc.vector, pv[2], list4, a2b2[:, 1, :])
+        fetch_pw(pw[0], 2)
+        fetch_pv(pv[1], 1)
+        scatter(nc.vector, pv[0], list4, b3[:])
+        fetch_pv(pv[2], 2)
+        gated = sbuf("gated", [P, PACK, O], F32)
+        nc.vector.tensor_tensor(out=gated[:], in0=first[:], in1=gate[:], op=ALU.mult)
+        fetch_pv(pv[0], 3)
+
+        hid = sbuf("hid", [P, O * PACK], BF16)
+        nc.vector.tensor_tensor(
+            out=hid[:].rearrange("p (c i t) -> p c t i", t=PACK, i=4),
+            in0=gated[:].rearrange("p t (c i) -> p c t i", i=4),
+            in1=second[:].rearrange("p t (c i) -> p c t i", i=4),
+            op=ALU.max,
+        )
+        hid_w = sbuf("hid_w", [P, O], U32)
+        hid_s = sbuf("hid_s", [P, O], U8)
+        nc.vector.quantize_mx(out=hid_w[:].bitcast(E5M2), scales=hid_s[:], in_=hid[:])
+
+        for h, (engine, queue) in enumerate(((nc.vector, nc.sync), (nc.scalar, nc.scalar))):
+            cols = slice(P * h, P * (h + 1))
+            bank = psum.tile([P, O], F32, name="y_bank%d" % h)
+            nc.tensor.matmul_mx(
+                out=bank[:],
+                lhsT=wb_w[:, cols].bitcast(E4M3),
+                lhsT_scale=wb_s[:, cols],
+                rhs=hid_w[:].bitcast(E5M2),
+                rhs_scale=hid_s[:],
+                start=True,
+                stop=True,
+            )
+            y = empty(engine, "y%d" % h, bank)
+            queue.dma_start(out[cols, :], y[:])

@@ -45,11 +45,9 @@ def tile_list_gatedboards_ahead_one_plain_kernel(
             queue.dma_start(tile[:].bitcast(I32), dram[0].rearrange("p c t -> p (c t)").bitcast(I32))
 
         def load_scale_rows(queue, plane, dram):
-            rows = dram[0].bitcast(I32)
-            for q in range(QUADS):
-                queue.dma_start(
-                    plane[QUAD * q : QUAD * q + PACK, :].bitcast(I32), rows[PACK * q : PACK * (q + 1), :]
-                )
+            rows = dram[0].bitcast(I32).rearrange("(q r) c -> r q c", r=PACK)
+            for r in range(PACK):
+                queue.dma_start(plane[r:P:QUAD, :].bitcast(I32), rows[r])
 
         def load_feature_vector(name, dram):
             tile = keep.tile([P, PACK], F32, name=name)
@@ -73,26 +71,31 @@ def tile_list_gatedboards_ahead_one_plain_kernel(
         w_w = sbuf("w_w", [P, R], U32)
         w_stage = sbuf("w_stage", [PACK, QUADS, R // 4], I32)
         w_s = sbuf("w_s", [P, R], U8)
-        w2_w = sbuf("w2_w", [P, R], U32)
+        w2_w = sbuf("w2_w", [P, R], U32, tag="w2_w_then_a1")
         w2_s = sbuf("w2_s", [P, R], U8, tag="w2_s_then_a0")
         wb_w = sbuf("wb_w", [P, N], U32)
         wb_s = sbuf("wb_s", [P, N], U8)
         pw = [sbuf("pw%d" % i, [P, C], F32) for i in range(2)]
-        pv = [sbuf("pv%d" % i, [P, C], F32) for i in range(3)]
+        pv = [sbuf("pv%d" % i, [P, C], F32) for i in range(4)]
 
-        for plane in (xt_s, w_s, w2_s, wb_s):
+        nc.gpsimd.memset(xt_s[:].bitcast(I32), 0)
+        warm_in = keep.tile([P, 1], F32, name="warm_in")
+        warm_out = keep.tile([P, 1], F32, name="warm_out")
+        nc.vector.memset(warm_in[:], 0.0)
+        nc.scalar.activation(out=warm_out[:], in_=warm_in[:], func=ACT.Sigmoid)
+        for plane in (w_s, w2_s, wb_s):
             nc.vector.memset(plane[:].bitcast(I32), 0)
-        for board in pw + pv:
-            nc.vector.memset(board[:], 0.0)
+        for board in [pw[1], pw[0]] + pv:
+            nc.gpsimd.memset(board[:], 0.0)
 
         nc.sync.dma_start(w_stage[:], w_scales[0].bitcast(I32).rearrange("(q r) c -> r q c", r=PACK))
         list1 = load_list("list1", offs)
         load_words(nc.sync, w_w, w_words)
+        load_scale_rows(nc.sync, xt_s, xt_scales)
         nc.sync.dma_start(xt_w[:].bitcast(I32), xt_words[0].bitcast(I32))
-        load_scale_rows(nc.scalar, xt_s, xt_scales)
         list2 = load_list("list2", offs2)
-        load_words(nc.sync, w2_w, w2_words)
         list3 = load_list("list3", offs3)
+        load_words(nc.sync, w2_w, w2_words)
         load_scale_rows(nc.sync, w2_s, w2_scales)
         list6 = load_list("list6", offs6)
         sg_t = load_feature_vector("sg_t", sg)
@@ -165,13 +168,12 @@ def tile_list_gatedboards_ahead_one_plain_kernel(
 
         a0_bank = psum.tile([P, J], F32, name="a0_bank")
         a1_bank = psum.tile([P, J], F32, name="a1_bank")
-        a3_bank = psum.tile([P, J], F32, name="a3_bank")
+        a23_bank = psum.tile([P, 2, J], F32, name="a23_bank")
         b01_bank = psum.tile([P, 2, J], F32, name="b01_bank")
-        b3_bank = psum.tile([P, J], F32, name="b3_bank")
-        a2b2_bank = psum.tile([P, 2, J], F32, name="a2b2_bank")
+        b23_bank = psum.tile([P, 2, J], F32, name="b23_bank")
 
         x1_w, x1_s = gather_tokens("x1", list1)
-        for t, rows in ((1, a1_bank[:]), (3, a3_bank[:]), (0, a0_bank[:]), (2, a2b2_bank[:, 0, :])):
+        for t, rows in ((1, a1_bank[:]), (0, a0_bank[:]), (2, a23_bank[:, 0, :]), (3, a23_bank[:, 1, :])):
             product(rows, t, w_dw, w_ds, E5M2, x1_w, x1_s)
 
         x2_w, x2_s = gather_tokens("x2", list2)
@@ -179,33 +181,32 @@ def tile_list_gatedboards_ahead_one_plain_kernel(
         w2_ds = sbuf("w2_ds", [P, R], U8)
         deal_words(w2_dw, w2_w)
         deal_scales(w2_ds, w2_s)
-        for t, rows in ((0, b01_bank[:, 0, :]), (1, b01_bank[:, 1, :]), (3, b3_bank[:]), (2, a2b2_bank[:, 1, :])):
-            product(rows, t, w2_dw, w2_ds, E4M3, x2_w, x2_s)
+        for t in range(PACK):
+            product((b01_bank, b23_bank)[t // 2][:, t % 2, :], t, w2_dw, w2_ds, E4M3, x2_w, x2_s)
 
-        a1 = empty(nc.scalar, "a1", a1_bank)
+        a1 = empty(nc.scalar, "a1", a1_bank, tag="w2_w_then_a1")
         scatter(nc.scalar, pw[1], list3, a1[:])
         a0 = empty(nc.vector, "a0", a0_bank, tag="w2_s_then_a0")
         scatter(nc.vector, pw[0], list3, a0[:])
         fetch_pw(pw[1], 1)
-        a3 = empty(nc.scalar, "a3", a3_bank)
-        scatter(nc.scalar, pw[1], list3, a3[:])
-        b01 = empty(nc.vector, "b01", b01_bank)
+        a23 = empty(nc.scalar, "a23", a23_bank, tag="w2_w_then_a1")
+        b23 = empty(nc.scalar, "b23", b23_bank)
+        scatter(nc.scalar, pw[1], list3, a23[:, 1, :])
+        b01 = empty(nc.vector, "b01", b01_bank, tag="w2_s_then_a0")
         scatter(nc.vector, pv[0], list4, b01[:, 0, :])
         fetch_pw(pw[1], 3)
         fetch_pw(pw[0], 0)
         scatter(nc.vector, pv[1], list4, b01[:, 1, :])
-        b3 = empty(nc.scalar, "b3", b3_bank)
-        a2b2 = empty(nc.scalar, "a2b2", a2b2_bank)
-        fetch_pv(pv[0], 0)
-        scatter(nc.scalar, pw[0], list3, a2b2[:, 0, :])
-        scatter(nc.vector, pv[2], list4, a2b2[:, 1, :])
+        scatter(nc.scalar, pw[0], list3, a23[:, 0, :])
+        scatter(nc.vector, pv[2], list4, b23[:, 0, :])
         fetch_pw(pw[0], 2)
+        fetch_pv(pv[0], 0)
         fetch_pv(pv[1], 1)
-        scatter(nc.vector, pv[0], list4, b3[:])
+        scatter(nc.vector, pv[3], list4, b23[:, 1, :])
         fetch_pv(pv[2], 2)
         gated = sbuf("gated", [P, PACK, O], F32)
         nc.vector.tensor_tensor(out=gated[:], in0=first[:], in1=gate[:], op=ALU.mult)
-        fetch_pv(pv[0], 3)
+        fetch_pv(pv[3], 3)
 
         hid = sbuf("hid", [P, O * PACK], BF16)
         nc.vector.tensor_tensor(

@@ -54,10 +54,10 @@ def tile_list_gatedboards_ahead_one_plain_kernel(
             nc.sync.dma_start(tile[:], dram.rearrange("(p t) one -> p (t one)", t=PACK))
             return tile
 
-        def deal_words(dealt, words):
+        def deal_words(dealt, words, slices):
             nc.scalar.copy(
-                out=dealt[:].rearrange("p (t c i) -> p c t i", t=PACK, i=4),
-                in_=words[:].rearrange("p (c i t) -> p c t i", t=PACK, i=4),
+                out=dealt[:].rearrange("p (t c i) -> p c t i", t=PACK, i=4)[:, :, slices, :],
+                in_=words[:].rearrange("p (c i t) -> p c t i", t=PACK, i=4)[:, :, slices, :],
             )
 
         def deal_scales(dealt, plane):
@@ -68,34 +68,36 @@ def tile_list_gatedboards_ahead_one_plain_kernel(
 
         xt_w = sbuf("xt_w", [P, T], U16)
         xt_s = sbuf("xt_s", [P, T], U8)
-        w_w = sbuf("w_w", [P, R], U32)
+        w_w = sbuf("w_w", [P, R], U32, tag="w_w_then_pv3")
         w_stage = sbuf("w_stage", [PACK, QUADS, R // 4], I32)
-        w_s = sbuf("w_s", [P, R], U8)
+        w_s = sbuf("w_s", [P, R], U8, tag="w_s_then_pv2")
         w2_w = sbuf("w2_w", [P, R], U32, tag="w2_w_then_a1")
         w2_s = sbuf("w2_s", [P, R], U8, tag="w2_s_then_a0")
         wb_w = sbuf("wb_w", [P, N], U32)
         wb_s = sbuf("wb_s", [P, N], U8)
         pw = [sbuf("pw%d" % i, [P, C], F32) for i in range(2)]
-        pv = [sbuf("pv%d" % i, [P, C], F32) for i in range(4)]
+        pv = [sbuf("pv%d" % i, [P, C], F32) for i in range(2)]
 
-        nc.gpsimd.memset(xt_s[:].bitcast(I32), 0)
+        nc.vector.memset(xt_s[:].bitcast(I32), 0)
         warm_in = keep.tile([P, 1], F32, name="warm_in")
         warm_out = keep.tile([P, 1], F32, name="warm_out")
         nc.vector.memset(warm_in[:], 0.0)
         nc.scalar.activation(out=warm_out[:], in_=warm_in[:], func=ACT.Sigmoid)
         for plane in (w_s, w2_s, wb_s):
             nc.vector.memset(plane[:].bitcast(I32), 0)
-        for board in [pw[1], pw[0]] + pv:
+        for board in (pw[1], pw[0]):
+            nc.vector.memset(board[:], 0.0)
+        for board in pv:
             nc.gpsimd.memset(board[:], 0.0)
 
         nc.sync.dma_start(w_stage[:], w_scales[0].bitcast(I32).rearrange("(q r) c -> r q c", r=PACK))
         list1 = load_list("list1", offs)
-        load_words(nc.sync, w_w, w_words)
-        load_scale_rows(nc.sync, xt_s, xt_scales)
         nc.sync.dma_start(xt_w[:].bitcast(I32), xt_words[0].bitcast(I32))
+        load_scale_rows(nc.sync, xt_s, xt_scales)
+        load_words(nc.sync, w_w, w_words)
         list2 = load_list("list2", offs2)
-        list3 = load_list("list3", offs3)
         load_words(nc.sync, w2_w, w2_words)
+        list3 = load_list("list3", offs3)
         load_scale_rows(nc.sync, w2_s, w2_scales)
         list6 = load_list("list6", offs6)
         sg_t = load_feature_vector("sg_t", sg)
@@ -113,13 +115,18 @@ def tile_list_gatedboards_ahead_one_plain_kernel(
         w_dw = sbuf("w_dw", [P, R], U32)
         w_ds = sbuf("w_ds", [P, R], U8)
         deal_scales(w_ds, w_s)
-        deal_words(w_dw, w_w)
+        deal_words(w_dw, w_w, slice(0, 2))
+        deal_words(w_dw, w_w, slice(2, 4))
+        pv.append(sbuf("pv2", [P, C], F32, tag="w_s_then_pv2"))
+        pv.append(sbuf("pv3", [P, C], F32, tag="w_w_then_pv3"))
+        for board in pv[2:]:
+            nc.gpsimd.memset(board[:], 0.0)
 
         def gather_tokens(name, offsets):
             words = sbuf(name + "_w", [P, J], U16)
             scales = sbuf(name + "_s", [P, J], U8)
-            nc.vector.tensor_copy(out=scales[:], in_=xt_s[:].indirect(offsets[:]))
             nc.vector.tensor_copy(out=words[:], in_=xt_w[:].indirect(offsets[:]))
+            nc.vector.tensor_copy(out=scales[:], in_=xt_s[:].indirect(offsets[:]))
             return words, scales
 
         def product(out_rows, t, words, scales, fmt, x_w, x_s):
@@ -179,41 +186,42 @@ def tile_list_gatedboards_ahead_one_plain_kernel(
         x2_w, x2_s = gather_tokens("x2", list2)
         w2_dw = sbuf("w2_dw", [P, R], U32)
         w2_ds = sbuf("w2_ds", [P, R], U8)
-        deal_words(w2_dw, w2_w)
+        deal_words(w2_dw, w2_w, slice(0, PACK))
         deal_scales(w2_ds, w2_s)
         for t in range(PACK):
             product((b01_bank, b23_bank)[t // 2][:, t % 2, :], t, w2_dw, w2_ds, E4M3, x2_w, x2_s)
 
-        a1 = empty(nc.scalar, "a1", a1_bank, tag="w2_w_then_a1")
+        a1 = empty(nc.scalar, "a1", a1_bank)
         scatter(nc.scalar, pw[1], list3, a1[:])
         a0 = empty(nc.vector, "a0", a0_bank, tag="w2_s_then_a0")
         scatter(nc.vector, pw[0], list3, a0[:])
         fetch_pw(pw[1], 1)
         a23 = empty(nc.scalar, "a23", a23_bank, tag="w2_w_then_a1")
-        b23 = empty(nc.scalar, "b23", b23_bank)
         scatter(nc.scalar, pw[1], list3, a23[:, 1, :])
-        b01 = empty(nc.vector, "b01", b01_bank, tag="w2_s_then_a0")
-        scatter(nc.vector, pv[0], list4, b01[:, 0, :])
+        b = sbuf("b", [P, PACK, J], F32, tag="w2_s_then_a0")
+        nc.vector.tensor_copy(out=b[:, 0:2, :], in_=b01_bank[:])
+        nc.scalar.copy(out=b[:, 2:4, :], in_=b23_bank[:])
+        scatter(nc.vector, pv[0], list4, b[:, 0, :])
         fetch_pw(pw[1], 3)
         fetch_pw(pw[0], 0)
-        scatter(nc.vector, pv[1], list4, b01[:, 1, :])
+        scatter(nc.vector, pv[1], list4, b[:, 1, :])
         scatter(nc.scalar, pw[0], list3, a23[:, 0, :])
-        scatter(nc.vector, pv[2], list4, b23[:, 0, :])
+        scatter(nc.vector, pv[2], list4, b[:, 2, :])
         fetch_pw(pw[0], 2)
         fetch_pv(pv[0], 0)
         fetch_pv(pv[1], 1)
-        scatter(nc.vector, pv[3], list4, b23[:, 1, :])
+        scatter(nc.vector, pv[3], list4, b[:, 3, :])
         fetch_pv(pv[2], 2)
         gated = sbuf("gated", [P, PACK, O], F32)
         nc.vector.tensor_tensor(out=gated[:], in0=first[:], in1=gate[:], op=ALU.mult)
         fetch_pv(pv[3], 3)
 
+        larger = sbuf("larger", [P, PACK, O], BF16)
+        nc.vector.tensor_tensor(out=larger[:], in0=gated[:], in1=second[:], op=ALU.max)
         hid = sbuf("hid", [P, O * PACK], BF16)
-        nc.vector.tensor_tensor(
+        nc.vector.tensor_copy(
             out=hid[:].rearrange("p (c i t) -> p c t i", t=PACK, i=4),
-            in0=gated[:].rearrange("p t (c i) -> p c t i", i=4),
-            in1=second[:].rearrange("p t (c i) -> p c t i", i=4),
-            op=ALU.max,
+            in_=larger[:].rearrange("p t (c i) -> p c t i", i=4),
         )
         hid_w = sbuf("hid_w", [P, O], U32)
         hid_s = sbuf("hid_s", [P, O], U8)

from contextlib import ExitStack

import concourse.mybir as mybir

K, T, J, R, C, O, N = 512, 2048, 256, 512, 512, 128, 256
FLOPS = 2 * (2 * K * R * J + R * N * O)

F32 = mybir.dt.float32
BF16 = mybir.dt.bfloat16
I32 = mybir.dt.int32
U32 = mybir.dt.uint32
U16 = mybir.dt.uint16
U8 = mybir.dt.uint8
E2M1 = mybir.dt.float4_e2m1fn_x4
E4M3 = mybir.dt.float8_e4m3fn_x4
E5M2 = mybir.dt.float8_e5m2_x4
ACT = mybir.ActivationFunctionType
ALU = mybir.AluOpType

P = 128
PACK = 4
QUADS = 4
QUAD = 32


def tile_list_gatedboards_ahead_one_plain_kernel(
    tc, xt_words, xt_scales, w_words, w_scales, w2_words, w2_scales, sa, sb, sg, bg,
    wb_words, wb_scales, offs, offs2, offs3, offs4, offs5, offs6, offs7, out,
):
    nc = tc.nc

    with ExitStack() as ctx:
        keep = ctx.enter_context(tc.tile_pool(name="keep", bufs=1))
        psum = ctx.enter_context(tc.psum_pool(name="psum", bufs=1))

        def sbuf(name, shape, dtype, tag=None):
            return keep.tile(shape, dtype, name=name, tag=tag or name, align_bytes=64)

        def load_list(name, dram):
            tile = keep.tile(list(dram.shape), U16, name=name)
            nc.sync.dma_start(tile[:], dram)
            return tile

        def load_words(queue, tile, dram):
            queue.dma_start(tile[:].bitcast(I32), dram[0].rearrange("p c t -> p (c t)").bitcast(I32))

        def load_scale_rows(queue, plane, dram):
            rows = dram[0].bitcast(I32).rearrange("(q r) c -> r q c", r=PACK)
            for r in range(PACK):
                queue.dma_start(plane[r:P:QUAD, :].bitcast(I32), rows[r])

        def load_feature_vector(name, dram):
            tile = keep.tile([P, PACK], F32, name=name)
            nc.sync.dma_start(tile[:], dram.rearrange("(p t) one -> p (t one)", t=PACK))
            return tile

        def deal_words(dealt, words, slices):
            nc.scalar.copy(
                out=dealt[:].rearrange("p (t c i) -> p c t i", t=PACK, i=4)[:, :, slices, :],
                in_=words[:].rearrange("p (c i t) -> p c t i", t=PACK, i=4)[:, :, slices, :],
            )

        def deal_scales(dealt, plane):
            nc.vector.tensor_copy(
                out=dealt[:].rearrange("p (t c i) -> p c t i", t=PACK, i=16),
                in_=plane[:].rearrange("p (c i t) -> p c t i", t=PACK, i=16),
            )

        xt_w = sbuf("xt_w", [P, T], U16)
        xt_s = sbuf("xt_s", [P, T], U8)
        w_w = sbuf("w_w", [P, R], U32, tag="w_w_then_pv3")
        w_stage = sbuf("w_stage", [PACK, QUADS, R // 4], I32)
        w_s = sbuf("w_s", [P, R], U8, tag="w_s_then_pv2")
        w2_w = sbuf("w2_w", [P, R], U32, tag="w2_w_then_a1")
        w2_s = sbuf("w2_s", [P, R], U8, tag="w2_s_then_a0")
        wb_w = sbuf("wb_w", [P, N], U32)
        wb_s = sbuf("wb_s", [P, N], U8)
        pw = [sbuf("pw%d" % i, [P, C], F32) for i in range(2)]
        pv = [sbuf("pv%d" % i, [P, C], F32) for i in range(2)]

        nc.vector.memset(xt_s[:].bitcast(I32), 0)
        warm_in = keep.tile([P, 1], F32, name="warm_in")
        warm_out = keep.tile([P, 1], F32, name="warm_out")
        nc.vector.memset(warm_in[:], 0.0)
        nc.scalar.activation(out=warm_out[:], in_=warm_in[:], func=ACT.Sigmoid)
        for plane in (w_s, w2_s, wb_s):
            nc.vector.memset(plane[:].bitcast(I32), 0)
        for board in (pw[1], pw[0]):
            nc.vector.memset(board[:], 0.0)
        for board in pv:
            nc.gpsimd.memset(board[:], 0.0)

        nc.sync.dma_start(w_stage[:], w_scales[0].bitcast(I32).rearrange("(q r) c -> r q c", r=PACK))
        list1 = load_list("list1", offs)
        nc.sync.dma_start(xt_w[:].bitcast(I32), xt_words[0].bitcast(I32))
        load_scale_rows(nc.sync, xt_s, xt_scales)
        load_words(nc.sync, w_w, w_words)
        list2 = load_list("list2", offs2)
        load_words(nc.sync, w2_w, w2_words)
        list3 = load_list("list3", offs3)
        load_scale_rows(nc.sync, w2_s, w2_scales)
        list6 = load_list("list6", offs6)
        sg_t = load_feature_vector("sg_t", sg)
        bg_t = load_feature_vector("bg_t", bg)
        list5 = load_list("list5", offs5)
        sa_t = load_feature_vector("sa_t", sa)
        list4 = load_list("list4", offs4)
        list7 = load_list("list7", offs7)
        sb_t = load_feature_vector("sb_t", sb)
        load_words(nc.sync, wb_w, wb_words)
        load_scale_rows(nc.sync, wb_s, wb_scales)

        for q in range(QUADS):
            nc.vector.tensor_copy(out=w_s[QUAD * q : QUAD * q + PACK, :].bitcast(I32), in_=w_stage[:, q, :])
        w_dw = sbuf("w_dw", [P, R], U32)
        w_ds = sbuf("w_ds", [P, R], U8)
        deal_scales(w_ds, w_s)
        deal_words(w_dw, w_w, slice(0, 2))
        deal_words(w_dw, w_w, slice(2, 4))
        pv.append(sbuf("pv2", [P, C], F32, tag="w_s_then_pv2"))
        pv.append(sbuf("pv3", [P, C], F32, tag="w_w_then_pv3"))
        for board in pv[2:]:
            nc.gpsimd.memset(board[:], 0.0)

        def gather_tokens(name, offsets):
            words = sbuf(name + "_w", [P, J], U16)
            scales = sbuf(name + "_s", [P, J], U8)
            nc.vector.tensor_copy(out=words[:], in_=xt_w[:].indirect(offsets[:]))
            nc.vector.tensor_copy(out=scales[:], in_=xt_s[:].indirect(offsets[:]))
            return words, scales

        def product(out_rows, t, words, scales, fmt, x_w, x_s):
            cols = slice(P * t, P * (t + 1))
            nc.tensor.matmul_mx(
                out=out_rows,
                lhsT=words[:, cols].bitcast(fmt),
                lhsT_scale=scales[:, cols],
                rhs=x_w[:].bitcast(E2M1),
                rhs_scale=x_s[:],
                start=True,
                stop=True,
            )

        def empty(engine, name, bank, tag=None):
            rows = sbuf(name, list(bank.shape), F32, tag=tag)
            if engine is nc.scalar:
                nc.scalar.copy(out=rows[:], in_=bank[:])
            else:
                nc.vector.tensor_copy(out=rows[:], in_=bank[:])
            return rows

        def scatter(engine, board, offsets, values):
            if engine is nc.scalar:
                nc.scalar.activation(out=board[:].indirect(offsets[:]), in_=values, func=ACT.Copy)
            else:
                nc.vector.tensor_copy(out=board[:].indirect(offsets[:]), in_=values)

        first = sbuf("first", [P, PACK, O], F32)
        gate = sbuf("gate", [P, PACK, O], F32)
        second = sbuf("second", [P, PACK, O], F32)

        def fetch_pw(board, t):
            nc.scalar.activation(
                out=gate[:, t, :], in_=board[:].indirect(list6[:]), func=ACT.Sigmoid,
                bias=bg_t[:, t : t + 1], scale=sg_t[:, t : t + 1],
            )
            nc.scalar.activation(
                out=first[:, t, :], in_=board[:].indirect(list5[:]), func=ACT.Copy, scale=sa_t[:, t : t + 1]
            )

        def fetch_pv(board, t):
            nc.scalar.activation(
                out=second[:, t, :], in_=board[:].indirect(list7[:]), func=ACT.Copy, scale=sb_t[:, t : t + 1]
            )

        a0_bank = psum.tile([P, J], F32, name="a0_bank")
        a1_bank = psum.tile([P, J], F32, name="a1_bank")
        a23_bank = psum.tile([P, 2, J], F32, name="a23_bank")
        b01_bank = psum.tile([P, 2, J], F32, name="b01_bank")
        b23_bank = psum.tile([P, 2, J], F32, name="b23_bank")

        x1_w, x1_s = gather_tokens("x1", list1)
        for t, rows in ((1, a1_bank[:]), (0, a0_bank[:]), (2, a23_bank[:, 0, :]), (3, a23_bank[:, 1, :])):
            product(rows, t, w_dw, w_ds, E5M2, x1_w, x1_s)

        x2_w, x2_s = gather_tokens("x2", list2)
        w2_dw = sbuf("w2_dw", [P, R], U32)
        w2_ds = sbuf("w2_ds", [P, R], U8)
        deal_words(w2_dw, w2_w, slice(0, PACK))
        deal_scales(w2_ds, w2_s)
        for t in range(PACK):
            product((b01_bank, b23_bank)[t // 2][:, t % 2, :], t, w2_dw, w2_ds, E4M3, x2_w, x2_s)

        a1 = empty(nc.scalar, "a1", a1_bank)
        scatter(nc.scalar, pw[1], list3, a1[:])
        a0 = empty(nc.vector, "a0", a0_bank, tag="w2_s_then_a0")
        scatter(nc.vector, pw[0], list3, a0[:])
        fetch_pw(pw[1], 1)
        a23 = empty(nc.scalar, "a23", a23_bank, tag="w2_w_then_a1")
        scatter(nc.scalar, pw[1], list3, a23[:, 1, :])
        b = sbuf("b", [P, PACK, J], F32, tag="w2_s_then_a0")
        nc.vector.tensor_copy(out=b[:, 0:2, :], in_=b01_bank[:])
        nc.scalar.copy(out=b[:, 2:4, :], in_=b23_bank[:])
        scatter(nc.vector, pv[0], list4, b[:, 0, :])
        fetch_pw(pw[1], 3)
        fetch_pw(pw[0], 0)
        scatter(nc.vector, pv[1], list4, b[:, 1, :])
        scatter(nc.scalar, pw[0], list3, a23[:, 0, :])
        scatter(nc.vector, pv[2], list4, b[:, 2, :])
        fetch_pw(pw[0], 2)
        fetch_pv(pv[0], 0)
        fetch_pv(pv[1], 1)
        scatter(nc.vector, pv[3], list4, b[:, 3, :])
        fetch_pv(pv[2], 2)
        gated = sbuf("gated", [P, PACK, O], F32)
        nc.vector.tensor_tensor(out=gated[:], in0=first[:], in1=gate[:], op=ALU.mult)
        fetch_pv(pv[3], 3)

        larger = sbuf("larger", [P, PACK, O], BF16)
        nc.vector.tensor_tensor(out=larger[:], in0=gated[:], in1=second[:], op=ALU.max)
        hid = sbuf("hid", [P, O * PACK], BF16)
        nc.vector.tensor_copy(
            out=hid[:].rearrange("p (c i t) -> p c t i", t=PACK, i=4),
            in_=larger[:].rearrange("p t (c i) -> p c t i", i=4),
        )
        hid_w = sbuf("hid_w", [P, O], U32)
        hid_s = sbuf("hid_s", [P, O], U8)
        nc.vector.quantize_mx(out=hid_w[:].bitcast(E5M2), scales=hid_s[:], in_=hid[:])

        for h, (engine, queue) in enumerate(((nc.vector, nc.sync), (nc.scalar, nc.scalar))):
            cols = slice(P * h, P * (h + 1))
            bank = psum.tile([P, O], F32, name="y_bank%d" % h)
            nc.tensor.matmul_mx(
                out=bank[:],
                lhsT=wb_w[:, cols].bitcast(E4M3),
                lhsT_scale=wb_s[:, cols],
                rhs=hid_w[:].bitcast(E5M2),
                rhs_scale=hid_s[:],
                start=True,
                stop=True,
            )
            y = empty(engine, "y%d" % h, bank)
            queue.dma_start(out[cols, :], y[:])
